import numpy as np, ml_dtypes
CORES = [40,64,80,88,96,104,120,144]
N = 8
import mx_ref
NC, WB = 512, 3
D = 2 * WB + 1
BF = ml_dtypes.bfloat16
def setup_inputs(rng):
    def f(*shape):
        return mx_ref.flush((rng.standard_normal(shape, dtype=np.float32) * np.exp2(rng.integers(-2, 3, shape[:-1] + (1,)))).astype(BF))
    return {"w": f(N, 128, D * 512), "x": f(N, 128, 4 * NC)}
def setup_inputs_blocks(rng):
    d = setup_inputs(rng)
    for k in ("w", "x"): d[k] = mx_ref.spread(d[k], rng, 2)
    return d
def setup_inputs_wide(rng):
    d = setup_inputs(rng)
    for k in ("w", "x"): d[k] = mx_ref.flush((d[k].astype(np.float32) * np.exp2(rng.integers(-8, 9, (N, 1, 1))).astype(np.float32)).astype(BF))
    return d
def setup_inputs_zeros(rng):
    d = setup_inputs(rng); v = d["x"].reshape(N, 128, -1, 4).copy()
    v[np.broadcast_to((rng.random((N, 1, v.shape[2], 1)) < 0.33), v.shape)] = 0
    d["x"] = v.reshape(d["x"].shape)
    return d
def reference(w, x):
    QX = [mx_ref.quantize(x[j]) for j in range(N)]
    y = np.zeros((N, 128, NC), np.float32)
    for r in range(N):
        for i in range(D):
            p = mx_ref.matmul(mx_ref.quantize(w[r][:, 512 * i:512 * i + 512]), QX[(r + i - WB) % N])
            y[r] = p if i == 0 else y[r] + p
    return {"y": y}

from concourse.bass import DstId, RemoteDMATransfer
from concourse.mybir import dt, ActivationFunctionType

WORLD = 256
WB = 3
D = 2 * WB + 1
NC = 512
HALF = NC // 2
CUT = 384
WCUT = 3 * 128

PIECES = {"b": ("q", 0, 192), "c": ("q", 192, 384), "a": ("q", 384, 512), "s": ("s", 0, 512), "q": ("q", 0, 512)}
ARRIVAL = [(True, 0), (False, 0), (False, 1), (True, 1), (False, 2), (True, 2)]

SCRATCH = {
    "xb": ("sbuf", [128, 4 * NC], "bfloat16"),
    "wb": ("sbuf", [128, D * 512], "bfloat16"),
    "xq": ("sbuf", [128, NC], "float8_e4m3fn_x4"),
    "xs": ("sbuf", [128, NC], "uint8"),
    "wq": ("sbuf", [128, D * 128], "float8_e4m3fn_x4"),
    "ws": ("sbuf", [128, D * 128], "uint8"),
    "lq": ("sbuf", [128, (D - 1) * NC], "float8_e4m3fn_x4"),
    "ls": ("sbuf", [128, (D - 1) * NC], "uint8"),
    "yb": ("sbuf", [128, NC], "float32"),
    "ps": ("psum", [128, 1024], "float32"),
}
SEMAPHORES = ["lx1", "lx2", "lw1", "lw2", "qx1", "qx2", "qw", "got", "sent", "mm0", "mm1", "cp0", "cp1", "st0", "st1"] \
    + ["arr%d" % j for j in range(8)]


def _bits(mask):
    return [1 << k for k in range(mask.bit_length()) if (mask >> k) & 1]


def _join(bs):
    m = 0
    for b in bs:
        m |= b
    return m


def _perms(l):
    if len(l) <= 1:
        return [list(l)]
    out = []
    for k in range(len(l)):
        for p in _perms(l[:k] + l[k + 1:]):
            out.append([l[k]] + p)
    return out


def _rounds(dests):
    n = len(dests)
    out = [None] * n
    used = {}

    def rec(j):
        if j == n:
            return True
        for p in _perms(dests[j]):
            if all((k, d) not in used for k, d in enumerate(p)):
                for k, d in enumerate(p):
                    used[(k, d)] = 1
                out[j] = p
                if rec(j + 1):
                    return True
                for k, d in enumerate(p):
                    used.pop((k, d))
        return False

    rec(0)
    return out


def _plan(cores, topo):
    n = len(cores)
    want = [[(j + d) % n for d in range(-WB, WB + 1) if d != 0] for j in range(n)]
    same = _rounds([[r for r in want[j] if topo.same_plane(cores[j], cores[r])] for j in range(n)])
    cross = _rounds([[r for r in want[j] if not topo.same_plane(cores[j], cores[r])] for j in range(n)])
    plans = []
    for j, c0 in enumerate(cores):
        chip = [c for c in range(WORLD)
                if c != c0 and topo.host(c) == topo.host(c0) and topo.chip(c) == topo.chip(c0)]
        port = [c for c in chip if all(topo.may_write(c, cores[r]) for r in cross[j])]
        far = [c for c in port if topo.die(c) != topo.die(c0)]
        near = [c for c in port if topo.die(c) == topo.die(c0)]
        hb, hc, ha, hs = far[0], far[1], near[0], near[1]
        on = _bits(topo.mask(c0, hb))
        off = _bits(topo.mask(c0, cores[same[j][0]]))
        hi = [b for b in on if b not in off]
        s1, s2, s3 = same[j]
        calls = [
            ("qx1", [("b", _join(on[0:8]), False, [hb]), ("c", _join(on[8:16]), False, [hc])]),
            ("qx2", [("a", _join(hi[0:4]), False, [ha]), ("s", _join(hi[4:8]), False, [hs]),
                     ("s", _join(off[0:4]), True, [s1, s2]), ("s", _join(off[4:6]), True, [s3]),
                     ("a", _join(off[6:8]), True, [s3])]),
            (None, [("q", _join(off), True, [s1, s2])]),
        ]
        helpers = {}
        for h, piece, dst in ((hb, "b", cross[j] + [s3]), (hc, "c", cross[j] + [s3]),
                              (ha, "a", cross[j]), (hs, "s", cross[j])):
            m = topo.mask(h, cores[dst[0]])
            for r in dst:
                m &= topo.mask(h, cores[r])
            helpers[h] = (piece, m, True, dst)
        plans.append({"same": same[j], "cross": cross[j], "calls": calls, "helpers": helpers})
    return plans


def _view(T, piece, slot):
    kind, lo, hi = PIECES[piece]
    if slot is None:
        return T.xq[:, lo:hi].bitcast(dt.uint8) if kind == "q" else T.xs[:, lo:hi]
    o = NC * slot
    return T.lq[:, o + lo:o + hi].bitcast(dt.uint8) if kind == "q" else T.ls[:, o + lo:o + hi]


def _slot(j, r, n):
    i = (j - r + WB) % n
    return i if i < WB else i - 1


def _fused(g, core, T, topo, cores, j, transfers):
    n = len(cores)
    trs, local = [], 0
    for piece, mask, to_ranks, dst in transfers:
        ids, aps = [], []
        for d in dst:
            rid, pid = topo.addr(cores[d] if to_ranks else d, core)
            ids.append(DstId(rid=rid, pnc=pid))
            aps.append(_view(T, piece, _slot(j, d, n) if to_ranks else None))
        trs.append(RemoteDMATransfer(dst_ids=ids, dma_engine_mask=mask,
                                     remote_sem=T.sem["arr%d" % j] if to_ranks else T.sem.got,
                                     srcs=[_view(T, piece, None)], dsts=aps))
        local += len(_bits(mask))
    g.remote_dma_fused(trs, local_sem=T.sem.sent)
    return local


def rank_program(g, core, T, topo):
    cores = list(T.cores)
    n = len(cores)
    plans = _plan(cores, topo)
    S = T.sem
    rank = T.rank_of(core)

    if rank is None:
        for j in range(n):
            if core in plans[j]["helpers"]:
                tr = plans[j]["helpers"][core]
                got = 0
                for _, trs in plans[j]["calls"]:
                    for _, mask, to_ranks, dst in trs:
                        if not to_ranks and core in dst:
                            got += len(_bits(mask))
                g.wait_ge(S.got, got)
                g.wait_ge(S.sent, _fused(g, core, T, topo, cores, j, [tr]))
        return

    r = rank
    g.sync.dma_start(T.xb[:, 0:4 * CUT], T.x[:, 0:4 * CUT]).then_inc(S.lx1, 16)
    g.scalar.dma_start(T.xb[:, 4 * CUT:4 * NC], T.x[:, 4 * CUT:4 * NC]).then_inc(S.lx2, 16)
    g.sync.dma_start(T.wb[:, 0:4 * WCUT], T.w[:, 0:4 * WCUT]).then_inc(S.lw1, 16)
    g.scalar.dma_start(T.wb[:, 4 * WCUT:D * 512], T.w[:, 4 * WCUT:D * 512]).then_inc(S.lw2, 16)

    v = g.vector
    v.wait_ge(S.lx1, 16)
    v.quantize_mx(T.xq[:, 0:CUT], T.xs[:, 0:CUT], T.xb[:, 0:4 * CUT]).then_inc(S.qx1, 1)
    v.wait_ge(S.lx2, 16)
    v.quantize_mx(T.xq[:, CUT:NC], T.xs[:, CUT:NC], T.xb[:, 4 * CUT:4 * NC]).then_inc(S.qx2, 1)
    v.wait_ge(S.lw1, 16)
    v.quantize_mx(T.wq[:, 0:WCUT], T.ws[:, 0:WCUT], T.wb[:, 0:4 * WCUT]).then_inc(S.qw, 1)
    v.wait_ge(S.lw2, 16)
    v.quantize_mx(T.wq[:, WCUT:D * 128], T.ws[:, WCUT:D * 128], T.wb[:, 4 * WCUT:D * 512]).then_inc(S.qw, 1)

    sent = 0
    for gate, trs in plans[r]["calls"]:
        if gate is not None:
            g.wait_ge(S[gate], 1)
        sent += _fused(g, core, T, topo, cores, r, trs)
    g.wait_ge(S.sent, sent)

    need, when = {}, {}
    for j in range(n):
        trs = [tr for _, call in plans[j]["calls"] for tr in call] + list(plans[j]["helpers"].values())
        c = sum(len(_bits(mask)) for _, mask, to_ranks, dst in trs if to_ranks and r in dst)
        if c:
            need[j] = c
            plane = r in plans[j]["same"]
            when[j] = ARRIVAL.index((plane, plans[j]["same" if plane else "cross"].index(r)))
    order = [r] + sorted(need, key=lambda j: when[j])

    t = g.tensor
    t.wait_ge(S.qx1, 1)
    t.wait_ge(S.qx2, 1)
    t.wait_ge(S.qw, 2)
    for k, j in enumerate(order):
        i = (j - r + WB) % n
        if j == r:
            cq, cs, o = T.xq, T.xs, 0
        else:
            t.wait_ge(S["arr%d" % j], need[j])
            cq, cs, o = T.lq, T.ls, NC * _slot(j, r, n)
        for h in range(2):
            lo = o + HALF * h
            mm = t.matmul_mx(T.ps[:, 512 * h:512 * h + HALF], T.wq[:, 128 * i:128 * i + 128],
                             T.ws[:, 128 * i:128 * i + 128], cq[:, lo:lo + HALF], cs[:, lo:lo + HALF],
                             k == 0, k == len(order) - 1)
            if k == len(order) - 1:
                mm.then_inc(S["mm%d" % h], 1)

    v.wait_ge(S.mm0, 1)
    v.tensor_copy(T.yb[:, 0:HALF], T.ps[:, 0:HALF]).then_inc(S.cp0, 1)
    g.sync.wait_ge(S.cp0, 1)
    g.sync.dma_start(T.y[:, 0:HALF], T.yb[:, 0:HALF]).then_inc(S.st0, 16)
    g.sync.wait_ge(S.st0, 16)
    g.scalar.wait_ge(S.mm1, 1)
    g.scalar.activation(T.yb[:, HALF:NC], T.ps[:, 512:512 + HALF], ActivationFunctionType.Copy).then_inc(S.cp1, 1)
    g.scalar.wait_ge(S.cp1, 1)
    g.scalar.dma_start(T.y[:, HALF:NC], T.yb[:, HALF:NC]).then_inc(S.st1, 16)
    g.scalar.wait_ge(S.st1, 16)
